import numpy as np
import ml_dtypes


def mxq(x, axis, fmt="e4m3"):
    dtype, down = {"e4m3": (ml_dtypes.float8_e4m3fn, 7), "e5m2": (ml_dtypes.float8_e5m2, 14)}[fmt]
    v = np.moveaxis(np.asarray(x, np.float32).astype(ml_dtypes.bfloat16).astype(np.float64), axis, -1)
    blocks = v.reshape(v.shape[:-1] + (-1, 32))
    amax = np.abs(blocks).max(-1, keepdims=True)
    byte = np.maximum(np.where(amax > 0, np.frexp(amax)[1] - 1 + 127, 0) - down, 1)
    scale = np.exp2(byte - 127.0)
    codes = (blocks / scale).astype(np.float32).astype(dtype).astype(np.float64)
    return np.moveaxis((codes * scale).reshape(v.shape), -1, axis)


WIDE = False


def mx_kscale(k, group=512):
    if not WIDE:
        return np.ones(k)
    levels = np.array([10, -10, 5, -5, 0])
    if group != 512:
        return np.exp2(np.random.permutation(np.resize(levels, k // group))).repeat(group)
    if k % 512:
        return np.exp2(np.random.permutation(np.resize(levels, k // 32))).repeat(32)
    a = np.empty((k // 512, 16))
    for p in range(k // 512):
        a[p, :8] = np.random.permutation(np.resize(levels, 8))
        for g in range(8):
            far = levels[np.abs(levels - a[p, g]) >= 10]
            a[p, g + 8] = far[np.random.randint(len(far))]
    return np.exp2(a.ravel()).repeat(32)


def f64(x):
    return np.asarray(x).astype(np.float64)


K, R, M, N = 1024, 256, 512, 512


def setup_inputs():
    n = np.random.standard_normal
    s = mx_kscale(K)[:, None]
    z = mx_kscale(R, 0)
    return {
        "x": (n((K, N)) * s).astype(np.float32),
        "w": (n((K, M)) / np.sqrt(K) / s).astype(np.float32),
        "a": (n((K, R)) / np.sqrt(K) / s * z).astype(np.float32),
        "bb": (n((R, M)) / np.sqrt(R) / z[:, None]).astype(np.float32),
        "b": (0.5 * n((M, 1))).astype(np.float32),
    }


def reference(x, w, a, bb, b):
    xq = mxq(f64(x), 0, "e4m3")
    z = mxq(f64(a), 0, "e4m3").T @ xq
    y = (mxq(f64(w), 0, "e4m3").T @ xq) + (mxq(f64(bb), 0, "e4m3").T @ mxq(z, 0, "e4m3"))
    y = y + f64(b)
    y = np.square(np.maximum(y, 0.0))
    return y

@@ -1,0 +1,177 @@
+from contextlib import ExitStack
+
+import concourse.mybir as mybir
+
+K, R, M, N = 1024, 256, 512, 512
+FLOPS = 2 * N * (K * R + K * M + R * M)
+F32 = mybir.dt.float32
+BF16 = mybir.dt.bfloat16
+U32 = mybir.dt.uint32
+U8 = mybir.dt.uint8
+FP8X4 = mybir.dt.float8_e4m3fn_x4
+ALU = mybir.AluOpType
+ACT = mybir.ActivationFunctionType
+P = 128
+LOADS = ["bb","a0","a1","x001","x101","x023","x123","w001","w101","w023","w12","w13"]
+ORDER = [["V","Cbb"],["S","cbb"],["V","qbb"],["V","Ca0"],["S","ca0"],["V","qa0"],["V","Ca1"],["S","ca1"],["V","qa1"],["S","cx001"],["V","Cx001"],["V","qx001"],["S","cx101"],["V","Cx101"],["V","qx101"],["S","cx023"],["V","Cx023"],["P","z0"],["V","qx023"],["S","cx123"],["V","Cx123"],["P","z1"],["S","ze0"],["V","qx123"],["S","cw001"],["V","Cw001"],["P","z2"],["S","ze1"],["V","zq0"],["V","qw001"],["P","z3"],["S","ze2"],["V","zq1"],["V","Cw101"],["P","l0"],["S","ze3"],["P","l1"],["V","zq2"],["V","qw101"],["S","le00"],["P","l2"],["V","zq3"],["V","Cw023"],["P","l3"],["S","cw023"],["V","Cw12"],["P","m0"],["S","le10"],["V","qw023"],["V","qw12"],["P","m1"],["S","le01"],["V","Cw13"],["V","a00"],["P","m2"],["S","le11"],["V","qw13"],["V","a01"],["S","r00"],["V","a10"],["P","m3"],["V","a20"],["S","r01"],["V","a11"],["V","r10"],["S","r11"],["V","a31"],["V","r20"],["S","r31"],["V","a21"],["V","a30"],["V","r21"],["V","r30"]]
+SPLIT = {"bb":160,"a0":160,"a1":160,"x001":160,"x101":160,"x023":160,"x123":160,"w001":192,"w101":256,"w023":192,"w12":128,"w13":128}
+BBHI_AFTER = "START"
+
+
+def tile_rows_lora_relu2_bias_kernel(tc, x, w, a, bb, b, out):
+    nc = tc.nc
+    with ExitStack() as ctx:
+        sb = ctx.enter_context(tc.tile_pool(name="sb", bufs=1))
+        ps = ctx.enter_context(tc.psum_pool(name="ps", bufs=1))
+        ctx.enter_context(tc.manual_schedule())
+
+        width = {}
+        raw = {}
+        grp = {}
+        codes = {}
+        scales = {}
+        xof = {}
+        wof = {}
+        for n in LOADS:
+            wd = 256 if n in ("bb", "a0", "a1") else 128 * (len(n) - 2)
+            width[n] = wd
+            cw = 320 if n[0] == "a" else wd
+            raw[n] = sb.tile([P, 4, wd], F32, name="raw_" + n, align_bytes=64)
+            grp[n] = sb.tile([P, wd, 4], BF16, name="grp_" + n, align_bytes=64)
+            codes[n] = sb.tile([P, cw], U32, name="codes_" + n, align_bytes=64)
+            scales[n] = sb.tile([P, cw], U8, name="scales_" + n, align_bytes=64)
+            if n[0] in "xw":
+                for i in range(2, len(n)):
+                    (xof if n[0] == "x" else wof).setdefault((int(n[1]), int(n[i])), (n, 128 * (i - 2)))
+        bias = sb.tile([P, 4], F32, name="bias")
+        zb = [sb.tile([P, 128, 4], BF16, name="zb%d" % c, align_bytes=64) for c in range(4)]
+        zc = [sb.tile([P, 128], U32, name="zc%d" % c, align_bytes=64) for c in range(4)]
+        zs = [sb.tile([P, 128], U8, name="zs%d" % c, align_bytes=64) for c in range(4)]
+        low = [[sb.tile([P, 2, 256], F32, name="low%d%d" % (h, nh)) for nh in range(2)] for h in range(2)]
+        ys = [[sb.tile([P, 256], F32, name="y%d%d" % (t, nh)) for nh in range(2)] for t in range(4)]
+        rs = [[sb.tile([P, 256], F32, name="r%d%d" % (t, nh)) for nh in range(2)] for t in range(4)]
+        os2 = [[sb.tile([P, 256], F32, name="o%d%d" % (t, nh)) for nh in range(2)] for t in range(4)]
+        whole = [ps.tile([P, 512], F32, name="whole%d" % c) for c in range(4)]
+        rowb = [[ps.tile([P, 512], F32, name="row%d%d" % (h, nh)) for nh in range(2)] for h in range(2)]
+
+        bbv = bb.rearrange("(p j) m -> p j m", j=4)
+
+        def load(n):
+            if n == "bb":
+                nc.sync.dma_start(out=raw[n][0:64, :, :], in_=bbv[:, :, 0:256])
+                return
+            src = {"a": a, "x": x, "w": w}[n[0]]
+            g = int(n[1])
+            c0 = 0 if n[0] == "a" else 128 * int(n[2])
+            nc.sync.dma_start(
+                out=raw[n][:],
+                in_=src[512 * g : 512 * (g + 1), c0 : c0 + width[n]].rearrange("(p j) c -> p j c", j=4),
+            )
+
+        def load_hi():
+            nc.scalar.dma_start(out=raw["bb"][64:128, 0:3, :], in_=bbv[:, 1:4, 256:512])
+            nc.scalar.dma_start(out=raw["bb"][64:128, 3, :], in_=bbv[:, 0, 256:512])
+            with nc.allow_non_contiguous_dma(reason="one bias a partition"):
+                nc.scalar.dma_start(out=bias[:], in_=b.rearrange("(t p) o -> p (t o)", p=P))
+            for n in LOADS[LOADS.index("bb") + 1 :]:
+                load(n)
+
+        for n in LOADS[: LOADS.index("bb") + 1]:
+            load(n)
+        if BBHI_AFTER == "START":
+            load_hi()
+
+        def eng_copy(e, dst, src):
+            if e == "V":
+                nc.vector.tensor_copy(out=dst, in_=src)
+            else:
+                nc.scalar.activation(out=dst, in_=src, func=ACT.Copy)
+
+        def cast(e, n, lo, hi):
+            if lo == hi:
+                return
+            if n[0] == "a":
+                dst = grp[n][:].rearrange("p (x m) j -> p m j x", x=4)[:, lo // 4 : hi // 4, :, :]
+                src = raw[n][:, :, lo:hi].rearrange("p j (m x) -> p m j x", x=4)
+            else:
+                dst = grp[n][:, lo:hi, :].rearrange("p (c i) j -> p c j i", i=4)
+                src = raw[n][:, :, lo:hi].rearrange("p j (c i) -> p c j i", i=4)
+            eng_copy(e, dst, src)
+
+        def quant(cd, sc, src):
+            nc.vector.quantize_mx(out=cd.bitcast(FP8X4), scales=sc, in_=src.rearrange("p c j -> p (c j)"))
+
+        def mm(o, lc, ls, rc, rsc, start, stop):
+            nc.tensor.matmul_mx(
+                out=o, lhsT=lc.bitcast(FP8X4), lhsT_scale=ls, rhs=rc.bitcast(FP8X4), rhs_scale=rsc,
+                start=start, stop=stop,
+            )
+
+        for e, s in ORDER:
+            k = s[0]
+            if k == "C":
+                cast("V", s[1:], 0, SPLIT[s[1:]])
+            elif k == "c":
+                cast("S", s[1:], SPLIT[s[1:]], width[s[1:]])
+            elif k == "q":
+                n = s[1:]
+                quant(codes[n][:, 0 : width[n]], scales[n][:, 0 : width[n]], grp[n][:])
+                if n[0] == "a":
+                    quant(codes[n][:, 256:320], scales[n][:, 256:320], grp[n][:, 0:64, :])
+            elif s[:2] == "ze":
+                c = int(s[2])
+                eng_copy(e, zb[c][:], whole[c][:].rearrange("p (x n) -> p n x", x=4))
+            elif s[:2] == "zq":
+                c = int(s[2])
+                quant(zc[c][:], zs[c][:], zb[c][:])
+            elif k == "z":
+                c = int(s[1])
+                for xx in range(4):
+                    for g in range(2):
+                        n, o = xof[g, c]
+                        an = "a%d" % g
+                        mm(whole[c][:, 128 * xx : 128 * xx + 128],
+                           codes[an][:, 64 * xx : 64 * xx + 128], scales[an][:, 64 * xx : 64 * xx + 128],
+                           codes[n][:, o : o + 128], scales[n][:, o : o + 128], g == 0, g == 1)
+            elif s[:2] == "le":
+                h = int(s[2])
+                nh = int(s[3])
+                eng_copy(e, low[h][nh][:].rearrange("p t n -> p (t n)"), rowb[h][nh][:])
+            elif k == "l":
+                c = int(s[1])
+                for tt in range(2):
+                    for h in range(2):
+                        rows = slice(64 * h, 64 * h + 64)
+                        o = 256 * tt + 128 * (c % 2)
+                        mm(rowb[h][c // 2][:, o : o + 128],
+                           codes["bb"][rows, 128 * tt : 128 * tt + 128], scales["bb"][rows, 128 * tt : 128 * tt + 128],
+                           zc[c][rows, :], zs[c][rows, :], True, True)
+            elif k == "m":
+                t = int(s[1])
+                for c in range(4):
+                    for g in range(2):
+                        n, o = xof[g, c]
+                        wn, wo = wof[g, t]
+                        mm(whole[t][:, 128 * c : 128 * c + 128],
+                           codes[wn][:, wo : wo + 128], scales[wn][:, wo : wo + 128],
+                           codes[n][:, o : o + 128], scales[n][:, o : o + 128], g == 0, g == 1)
+            elif k == "a":
+                t = int(s[1])
+                nh = int(s[2])
+                nc.vector.scalar_tensor_tensor(
+                    out=ys[t][nh][:], in0=whole[t][:, 256 * nh : 256 * nh + 256], scalar=bias[:, t : t + 1],
+                    in1=low[t // 2][nh][:, t % 2, :], op0=ALU.add, op1=ALU.add,
+                )
+            elif k == "r":
+                t = int(s[1])
+                nh = int(s[2])
+                if e == "V":
+                    nc.vector.scalar_tensor_tensor(
+                        out=os2[t][nh][:], in0=ys[t][nh][:], scalar=0.0, in1=ys[t][nh][:], op0=ALU.max, op1=ALU.mult
+                    )
+                else:
+                    nc.scalar.activation(out=rs[t][nh][:], in_=ys[t][nh][:], func=ACT.Relu)
+                    nc.scalar.activation(out=os2[t][nh][:], in_=rs[t][nh][:], func=ACT.Square)
+                nc.sync.dma_start(out=out[128 * t : 128 * t + 128, 256 * nh : 256 * nh + 256], in_=os2[t][nh][:])
+            if s == BBHI_AFTER:
+                load_hi()

@@ -13,8 +13,8 @@ ALU = mybir.AluOpType
 ACT = mybir.ActivationFunctionType
 P = 128
 LOADS = ["bb","a0","a1","x001","x101","x023","x123","w001","w101","w023","w12","w13"]
-ORDER = [["V","Cbb"],["S","cbb"],["V","qbb"],["V","Ca0"],["S","ca0"],["V","qa0"],["V","Ca1"],["S","ca1"],["V","qa1"],["S","cx001"],["V","Cx001"],["V","qx001"],["S","cx101"],["V","Cx101"],["V","qx101"],["S","cx023"],["V","Cx023"],["P","z0"],["V","qx023"],["S","cx123"],["V","Cx123"],["P","z1"],["S","ze0"],["V","qx123"],["S","cw001"],["V","Cw001"],["P","z2"],["S","ze1"],["V","zq0"],["V","qw001"],["P","z3"],["S","ze2"],["V","zq1"],["V","Cw101"],["P","l0"],["S","ze3"],["P","l1"],["V","zq2"],["V","qw101"],["S","le00"],["P","l2"],["V","zq3"],["V","Cw023"],["P","l3"],["S","cw023"],["V","Cw12"],["P","m0"],["S","le10"],["V","qw023"],["V","qw12"],["P","m1"],["S","le01"],["V","Cw13"],["V","a00"],["P","m2"],["S","le11"],["V","qw13"],["V","a01"],["S","r00"],["V","a10"],["P","m3"],["V","a20"],["S","r01"],["V","a11"],["V","r10"],["S","r11"],["V","a31"],["V","r20"],["S","r31"],["V","a21"],["V","a30"],["V","r21"],["V","r30"]]
-SPLIT = {"bb":160,"a0":160,"a1":160,"x001":160,"x101":160,"x023":160,"x123":160,"w001":192,"w101":256,"w023":192,"w12":128,"w13":128}
+ORDER = [["S","ca0"],["V","Ca0"],["V","Cbb"],["V","qa0"],["V","qbb"],["S","ca1"],["V","Ca1"],["V","qa1"],["S","cx001"],["V","Cx001"],["V","qx001"],["S","cx101"],["V","Cx101"],["V","qx101"],["S","cx023"],["V","Cx023"],["P","z0"],["V","qx023"],["S","cx123"],["V","Cx123"],["P","z1"],["S","ze0"],["V","qx123"],["S","cw001"],["V","Cw001"],["P","z2"],["S","ze1"],["V","zq0"],["V","qw001"],["P","z3"],["S","ze2"],["V","zq1"],["V","Cw101"],["P","l0"],["S","ze3"],["P","l1"],["V","zq2"],["V","qw101"],["S","le00"],["P","l2"],["V","zq3"],["V","Cw023"],["S","le10"],["P","l3"],["P","m0"],["V","Cw12"],["S","le01"],["V","qw023"],["P","m1"],["V","qw12"],["V","a00"],["S","le11"],["P","m2"],["V","a01"],["S","cw13"],["V","Cw13"],["V","a10"],["V","r01"],["S","r00"],["V","qw13"],["V","a11"],["P","m3"],["S","r10"],["V","a20"],["V","a21"],["S","r11"],["V","r20"],["V","a31"],["S","r21"],["V","a30"],["V","r31"],["V","r30"]]
+SPLIT = {"bb":256,"a0":128,"a1":96,"x001":128,"x101":160,"x023":160,"x123":160,"w001":224,"w101":256,"w023":256,"w12":128,"w13":64}
 BBHI_AFTER = "START"
 
 

@@ -4,6 +4,7 @@ import concourse.mybir as mybir
 
 K, R, M, N = 1024, 256, 512, 512
 FLOPS = 2 * N * (K * R + K * M + R * M)
+
 F32 = mybir.dt.float32
 BF16 = mybir.dt.bfloat16
 U32 = mybir.dt.uint32
@@ -11,11 +12,17 @@ U8 = mybir.dt.uint8
 FP8X4 = mybir.dt.float8_e4m3fn_x4
 ALU = mybir.AluOpType
 ACT = mybir.ActivationFunctionType
+
 P = 128
-LOADS = ["bb","a0","a1","x001","x101","x023","x123","w001","w101","w023","w12","w13"]
-ORDER = [["S","ca0"],["V","Ca0"],["V","Cbb"],["V","qa0"],["V","qbb"],["S","ca1"],["V","Ca1"],["V","qa1"],["S","cx001"],["V","Cx001"],["V","qx001"],["S","cx101"],["V","Cx101"],["V","qx101"],["S","cx023"],["V","Cx023"],["P","z0"],["V","qx023"],["S","cx123"],["V","Cx123"],["P","z1"],["S","ze0"],["V","qx123"],["S","cw001"],["V","Cw001"],["P","z2"],["S","ze1"],["V","zq0"],["V","qw001"],["P","z3"],["S","ze2"],["V","zq1"],["V","Cw101"],["P","l0"],["S","ze3"],["P","l1"],["V","zq2"],["V","qw101"],["S","le00"],["P","l2"],["V","zq3"],["V","Cw023"],["S","le10"],["P","l3"],["P","m0"],["V","Cw12"],["S","le01"],["V","qw023"],["P","m1"],["V","qw12"],["V","a00"],["S","le11"],["P","m2"],["V","a01"],["S","cw13"],["V","Cw13"],["V","a10"],["V","r01"],["S","r00"],["V","qw13"],["V","a11"],["P","m3"],["S","r10"],["V","a20"],["V","a21"],["S","r11"],["V","r20"],["V","a31"],["S","r21"],["V","a30"],["V","r31"],["V","r30"]]
-SPLIT = {"bb":256,"a0":128,"a1":96,"x001":128,"x101":160,"x023":160,"x123":160,"w001":224,"w101":256,"w023":256,"w12":128,"w13":64}
-BBHI_AFTER = "START"
+ROWS = 64
+PACK = 4
+K_PASS = P * PACK
+T = 128
+HALF = 256
+
+X_PIECES = ((0, 0, HALF, 128), (1, 0, HALF, 160), (0, HALF, HALF, 160), (1, HALF, HALF, 160))
+W_PIECES = ((0, 0, HALF, 192), (1, 0, HALF, HALF), (0, HALF, HALF, HALF), (1, HALF, T, T), (1, HALF + T, T, 0))
+BB_ON_VECTOR = 96
 
 
 def tile_rows_lora_relu2_bias_kernel(tc, x, w, a, bb, b, out):
@@ -25,153 +32,229 @@ def tile_rows_lora_relu2_bias_kernel(tc, x, w, a, bb, b, out):
         ps = ctx.enter_context(tc.psum_pool(name="ps", bufs=1))
         ctx.enter_context(tc.manual_schedule())
 
-        width = {}
-        raw = {}
-        grp = {}
-        codes = {}
-        scales = {}
-        xof = {}
-        wof = {}
-        for n in LOADS:
-            wd = 256 if n in ("bb", "a0", "a1") else 128 * (len(n) - 2)
-            width[n] = wd
-            cw = 320 if n[0] == "a" else wd
-            raw[n] = sb.tile([P, 4, wd], F32, name="raw_" + n, align_bytes=64)
-            grp[n] = sb.tile([P, wd, 4], BF16, name="grp_" + n, align_bytes=64)
-            codes[n] = sb.tile([P, cw], U32, name="codes_" + n, align_bytes=64)
-            scales[n] = sb.tile([P, cw], U8, name="scales_" + n, align_bytes=64)
-            if n[0] in "xw":
-                for i in range(2, len(n)):
-                    (xof if n[0] == "x" else wof).setdefault((int(n[1]), int(n[i])), (n, 128 * (i - 2)))
-        bias = sb.tile([P, 4], F32, name="bias")
-        zb = [sb.tile([P, 128, 4], BF16, name="zb%d" % c, align_bytes=64) for c in range(4)]
-        zc = [sb.tile([P, 128], U32, name="zc%d" % c, align_bytes=64) for c in range(4)]
-        zs = [sb.tile([P, 128], U8, name="zs%d" % c, align_bytes=64) for c in range(4)]
-        low = [[sb.tile([P, 2, 256], F32, name="low%d%d" % (h, nh)) for nh in range(2)] for h in range(2)]
-        ys = [[sb.tile([P, 256], F32, name="y%d%d" % (t, nh)) for nh in range(2)] for t in range(4)]
-        rs = [[sb.tile([P, 256], F32, name="r%d%d" % (t, nh)) for nh in range(2)] for t in range(4)]
-        os2 = [[sb.tile([P, 256], F32, name="o%d%d" % (t, nh)) for nh in range(2)] for t in range(4)]
-        whole = [ps.tile([P, 512], F32, name="whole%d" % c) for c in range(4)]
-        rowb = [[ps.tile([P, 512], F32, name="row%d%d" % (h, nh)) for nh in range(2)] for h in range(2)]
+        def operand(name, width, code_width):
+            return {
+                "width": width,
+                "raw": sb.tile([P, PACK, width], F32, name=name + "_raw", align_bytes=64),
+                "bf16": sb.tile([P, width, PACK], BF16, name=name + "_bf16", align_bytes=64),
+                "codes": sb.tile([P, code_width], U32, name=name + "_codes", align_bytes=64),
+                "scales": sb.tile([P, code_width], U8, name=name + "_scales", align_bytes=64),
+            }
 
-        bbv = bb.rearrange("(p j) m -> p j m", j=4)
+        bbq = operand("bb", HALF, HALF)
+        aq = [operand("a%d" % g, R, R + ROWS) for g in range(2)]
+        xq = [operand("x%d" % i, piece[2], piece[2]) for i, piece in enumerate(X_PIECES)]
+        wq = [operand("w%d" % i, piece[2], piece[2]) for i, piece in enumerate(W_PIECES)]
+        bias = sb.tile([P, M // T], F32, name="bias")
+        z_bf16 = [sb.tile([P, T, PACK], BF16, name="z_bf16_%d" % c, align_bytes=64) for c in range(N // T)]
+        z_codes = [sb.tile([P, T], U32, name="z_codes_%d" % c, align_bytes=64) for c in range(N // T)]
+        z_scales = [sb.tile([P, T], U8, name="z_scales_%d" % c, align_bytes=64) for c in range(N // T)]
+        branch = [[sb.tile([P, 2, HALF], F32, name="branch%d%d" % (h, u)) for u in range(2)] for h in range(2)]
+        y = [[sb.tile([P, HALF], F32, name="y%d%d" % (t, u)) for u in range(2)] for t in range(M // T)]
+        relu = [[sb.tile([P, HALF], F32, name="relu%d%d" % (t, u)) for u in range(2)] for t in range(2)]
+        res = [[sb.tile([P, HALF], F32, name="res%d%d" % (t, u)) for u in range(2)] for t in range(M // T)]
+        whole_bank = [ps.tile([P, N], F32, name="whole%d" % c) for c in range(4)]
+        half_bank = [[ps.tile([P, N], F32, name="half%d%d" % (h, u)) for u in range(2)] for h in range(2)]
 
-        def load(n):
-            if n == "bb":
-                nc.sync.dma_start(out=raw[n][0:64, :, :], in_=bbv[:, :, 0:256])
-                return
-            src = {"a": a, "x": x, "w": w}[n[0]]
-            g = int(n[1])
-            c0 = 0 if n[0] == "a" else 128 * int(n[2])
-            nc.sync.dma_start(
-                out=raw[n][:],
-                in_=src[512 * g : 512 * (g + 1), c0 : c0 + width[n]].rearrange("(p j) c -> p j c", j=4),
-            )
+        bb_rows = bb.rearrange("(p j) m -> p j m", j=PACK)
+        nc.sync.dma_start(out=bbq["raw"][0:ROWS, :, :], in_=bb_rows[:, :, 0:HALF])
+        nc.scalar.dma_start(out=bbq["raw"][ROWS:P, 0:3, :], in_=bb_rows[:, 1:4, HALF:M])
+        nc.scalar.dma_start(out=bbq["raw"][ROWS:P, 3, :], in_=bb_rows[:, 0, HALF:M])
 
-        def load_hi():
-            nc.scalar.dma_start(out=raw["bb"][64:128, 0:3, :], in_=bbv[:, 1:4, 256:512])
-            nc.scalar.dma_start(out=raw["bb"][64:128, 3, :], in_=bbv[:, 0, 256:512])
-            with nc.allow_non_contiguous_dma(reason="one bias a partition"):
-                nc.scalar.dma_start(out=bias[:], in_=b.rearrange("(t p) o -> p (t o)", p=P))
-            for n in LOADS[LOADS.index("bb") + 1 :]:
-                load(n)
+        def load(op, src, g, col):
+            rows = src[K_PASS * g : K_PASS * (g + 1), col : col + op["width"]]
+            nc.sync.dma_start(out=op["raw"][:], in_=rows.rearrange("(p j) c -> p j c", j=PACK))
 
-        for n in LOADS[: LOADS.index("bb") + 1]:
-            load(n)
-        if BBHI_AFTER == "START":
-            load_hi()
+        for g in range(2):
+            load(aq[g], a, g, 0)
+        for op, piece in zip(xq, X_PIECES):
+            load(op, x, piece[0], piece[1])
+        for op, piece in zip(wq, W_PIECES):
+            load(op, w, piece[0], piece[1])
+        with nc.allow_non_contiguous_dma(reason="one bias for each partition of an output tile"):
+            nc.sync.dma_start(out=bias[:], in_=b.rearrange("(t p) o -> p (t o)", p=P))
 
-        def eng_copy(e, dst, src):
-            if e == "V":
+        def scalar_copy(dst, src):
+            nc.scalar.activation(out=dst, in_=src, func=ACT.Copy)
+
+        def cast_views(op, lo, hi):
+            dst = op["bf16"][:, lo:hi, :].rearrange("p (c i) j -> p c j i", i=2)
+            src = op["raw"][:, :, lo:hi].rearrange("p j (c i) -> p c j i", i=2)
+            return dst, src
+
+        def cast(op, on_vector):
+            if on_vector < op["width"]:
+                scalar_copy(*cast_views(op, on_vector, op["width"]))
+            if on_vector > 0:
+                dst, src = cast_views(op, 0, on_vector)
                 nc.vector.tensor_copy(out=dst, in_=src)
-            else:
-                nc.scalar.activation(out=dst, in_=src, func=ACT.Copy)
 
-        def cast(e, n, lo, hi):
-            if lo == hi:
-                return
-            if n[0] == "a":
-                dst = grp[n][:].rearrange("p (x m) j -> p m j x", x=4)[:, lo // 4 : hi // 4, :, :]
-                src = raw[n][:, :, lo:hi].rearrange("p j (m x) -> p m j x", x=4)
-            else:
-                dst = grp[n][:, lo:hi, :].rearrange("p (c i) j -> p c j i", i=4)
-                src = raw[n][:, :, lo:hi].rearrange("p j (c i) -> p c j i", i=4)
-            eng_copy(e, dst, src)
+        def cast_a(g):
+            dst = aq[g]["bf16"][:].rearrange("p (group m) j -> p m j group", group=PACK)
+            src = aq[g]["raw"][:].rearrange("p j (m group) -> p m j group", group=PACK)
+            scalar_copy(dst[:, :, :, 2:4], src[:, :, :, 2:4])
+            nc.vector.tensor_copy(out=dst[:, :, :, 0:2], in_=src[:, :, :, 0:2])
 
-        def quant(cd, sc, src):
-            nc.vector.quantize_mx(out=cd.bitcast(FP8X4), scales=sc, in_=src.rearrange("p c j -> p (c j)"))
+        def quantize(codes, scales, src):
+            nc.vector.quantize_mx(out=codes.bitcast(FP8X4), scales=scales, in_=src.rearrange("p c j -> p (c j)"))
 
-        def mm(o, lc, ls, rc, rsc, start, stop):
+        def quantize_piece(op):
+            quantize(op["codes"][:], op["scales"][:], op["bf16"][:])
+
+        def quantize_a(g):
+            op = aq[g]
+            quantize(op["codes"][:, 0:R], op["scales"][:, 0:R], op["bf16"][:])
+            quantize(op["codes"][:, R : R + ROWS], op["scales"][:, R : R + ROWS], op["bf16"][:, 0:ROWS, :])
+
+        def quantize_z(c):
+            quantize(z_codes[c][:], z_scales[c][:], z_bf16[c][:])
+
+        def window(ops, pieces, g, col):
+            for op, piece in zip(ops, pieces):
+                if piece[0] == g and piece[1] <= col < piece[1] + piece[2]:
+                    cols = slice(col - piece[1], col - piece[1] + T)
+                    return op["codes"][:, cols], op["scales"][:, cols]
+            raise ValueError("no piece holds these columns")
+
+        def matmul(dst, stationary, moving, start, stop):
             nc.tensor.matmul_mx(
-                out=o, lhsT=lc.bitcast(FP8X4), lhsT_scale=ls, rhs=rc.bitcast(FP8X4), rhs_scale=rsc,
-                start=start, stop=stop,
+                out=dst,
+                lhsT=stationary[0].bitcast(FP8X4),
+                lhsT_scale=stationary[1],
+                rhs=moving[0].bitcast(FP8X4),
+                rhs_scale=moving[1],
+                start=start,
+                stop=stop,
             )
 
-        for e, s in ORDER:
-            k = s[0]
-            if k == "C":
-                cast("V", s[1:], 0, SPLIT[s[1:]])
-            elif k == "c":
-                cast("S", s[1:], SPLIT[s[1:]], width[s[1:]])
-            elif k == "q":
-                n = s[1:]
-                quant(codes[n][:, 0 : width[n]], scales[n][:, 0 : width[n]], grp[n][:])
-                if n[0] == "a":
-                    quant(codes[n][:, 256:320], scales[n][:, 256:320], grp[n][:, 0:64, :])
-            elif s[:2] == "ze":
-                c = int(s[2])
-                eng_copy(e, zb[c][:], whole[c][:].rearrange("p (x n) -> p n x", x=4))
-            elif s[:2] == "zq":
-                c = int(s[2])
-                quant(zc[c][:], zs[c][:], zb[c][:])
-            elif k == "z":
-                c = int(s[1])
-                for xx in range(4):
-                    for g in range(2):
-                        n, o = xof[g, c]
-                        an = "a%d" % g
-                        mm(whole[c][:, 128 * xx : 128 * xx + 128],
-                           codes[an][:, 64 * xx : 64 * xx + 128], scales[an][:, 64 * xx : 64 * xx + 128],
-                           codes[n][:, o : o + 128], scales[n][:, o : o + 128], g == 0, g == 1)
-            elif s[:2] == "le":
-                h = int(s[2])
-                nh = int(s[3])
-                eng_copy(e, low[h][nh][:].rearrange("p t n -> p (t n)"), rowb[h][nh][:])
-            elif k == "l":
-                c = int(s[1])
-                for tt in range(2):
-                    for h in range(2):
-                        rows = slice(64 * h, 64 * h + 64)
-                        o = 256 * tt + 128 * (c % 2)
-                        mm(rowb[h][c // 2][:, o : o + 128],
-                           codes["bb"][rows, 128 * tt : 128 * tt + 128], scales["bb"][rows, 128 * tt : 128 * tt + 128],
-                           zc[c][rows, :], zs[c][rows, :], True, True)
-            elif k == "m":
-                t = int(s[1])
-                for c in range(4):
-                    for g in range(2):
-                        n, o = xof[g, c]
-                        wn, wo = wof[g, t]
-                        mm(whole[t][:, 128 * c : 128 * c + 128],
-                           codes[wn][:, wo : wo + 128], scales[wn][:, wo : wo + 128],
-                           codes[n][:, o : o + 128], scales[n][:, o : o + 128], g == 0, g == 1)
-            elif k == "a":
-                t = int(s[1])
-                nh = int(s[2])
-                nc.vector.scalar_tensor_tensor(
-                    out=ys[t][nh][:], in0=whole[t][:, 256 * nh : 256 * nh + 256], scalar=bias[:, t : t + 1],
-                    in1=low[t // 2][nh][:, t % 2, :], op0=ALU.add, op1=ALU.add,
-                )
-            elif k == "r":
-                t = int(s[1])
-                nh = int(s[2])
-                if e == "V":
-                    nc.vector.scalar_tensor_tensor(
-                        out=os2[t][nh][:], in0=ys[t][nh][:], scalar=0.0, in1=ys[t][nh][:], op0=ALU.max, op1=ALU.mult
+        def z_product(c):
+            for j in range(PACK):
+                cols = slice(ROWS * j, ROWS * j + T)
+                for g in range(2):
+                    a_window = (aq[g]["codes"][:, cols], aq[g]["scales"][:, cols])
+                    matmul(whole_bank[c][:, T * j : T * (j + 1)], a_window, window(xq, X_PIECES, g, T * c), g == 0, g == 1)
+
+        def z_out(c):
+            scalar_copy(z_bf16[c][:], whole_bank[c][:].rearrange("p (j n) -> p n j", j=PACK))
+
+        def branch_product(c):
+            for tile in range(2):
+                cols = slice(T * tile, T * (tile + 1))
+                at = HALF * tile + T * (c % 2)
+                for h in range(2):
+                    rows = slice(ROWS * h, ROWS * (h + 1))
+                    matmul(
+                        half_bank[h][c // 2][:, at : at + T],
+                        (bbq["codes"][rows, cols], bbq["scales"][rows, cols]),
+                        (z_codes[c][rows, :], z_scales[c][rows, :]),
+                        True,
+                        True,
                     )
-                else:
-                    nc.scalar.activation(out=rs[t][nh][:], in_=ys[t][nh][:], func=ACT.Relu)
-                    nc.scalar.activation(out=os2[t][nh][:], in_=rs[t][nh][:], func=ACT.Square)
-                nc.sync.dma_start(out=out[128 * t : 128 * t + 128, 256 * nh : 256 * nh + 256], in_=os2[t][nh][:])
-            if s == BBHI_AFTER:
-                load_hi()
+
+        def branch_out(h, u):
+            scalar_copy(branch[h][u][:].rearrange("p t n -> p (t n)"), half_bank[h][u][:])
+
+        def main_product(t):
+            for c in range(N // T):
+                for g in range(2):
+                    matmul(
+                        whole_bank[t][:, T * c : T * (c + 1)],
+                        window(wq, W_PIECES, g, T * t),
+                        window(xq, X_PIECES, g, T * c),
+                        g == 0,
+                        g == 1,
+                    )
+
+        def add_up(t, u):
+            nc.vector.scalar_tensor_tensor(
+                out=y[t][u][:],
+                in0=whole_bank[t][:, HALF * u : HALF * (u + 1)],
+                scalar=bias[:, t : t + 1],
+                in1=branch[t // 2][u][:, t % 2, :],
+                op0=ALU.add,
+                op1=ALU.add,
+            )
+
+        def store(t, u):
+            nc.sync.dma_start(out=out[T * t : T * (t + 1), HALF * u : HALF * (u + 1)], in_=res[t][u][:])
+
+        def relu_on_scalar(t, u):
+            nc.scalar.activation(out=relu[t][u][:], in_=y[t][u][:], func=ACT.Relu)
+
+        def square_on_scalar(t, u):
+            nc.scalar.activation(out=res[t][u][:], in_=relu[t][u][:], func=ACT.Square)
+            store(t, u)
+
+        def finish_on_vector(t, u):
+            nc.vector.scalar_tensor_tensor(
+                out=res[t][u][:], in0=y[t][u][:], scalar=0.0, in1=y[t][u][:], op0=ALU.max, op1=ALU.mult
+            )
+            store(t, u)
+
+        cast_a(0)
+        cast(bbq, BB_ON_VECTOR)
+        quantize_a(0)
+        cast_a(1)
+        quantize_piece(bbq)
+        cast(xq[0], X_PIECES[0][3])
+        quantize_a(1)
+        quantize_piece(xq[0])
+        cast(xq[1], X_PIECES[1][3])
+        quantize_piece(xq[1])
+        z_product(0)
+        z_product(1)
+        for i in (2, 3):
+            cast(xq[i], X_PIECES[i][3])
+            quantize_piece(xq[i])
+        z_product(2)
+        z_product(3)
+
+        z_out(0)
+        cast(wq[0], W_PIECES[0][3])
+        z_out(1)
+        quantize_z(0)
+        quantize_piece(wq[0])
+        z_out(2)
+        quantize_z(1)
+        cast(wq[1], W_PIECES[1][3])
+        branch_product(0)
+        branch_product(1)
+        z_out(3)
+        quantize_z(2)
+        quantize_piece(wq[1])
+        branch_product(2)
+        quantize_z(3)
+        branch_product(3)
+
+        for u in range(2):
+            for h in range(2):
+                branch_out(h, u)
+        cast(wq[2], W_PIECES[2][3])
+        cast(wq[3], W_PIECES[3][3])
+        quantize_piece(wq[2])
+        quantize_piece(wq[3])
+        for t in range(3):
+            main_product(t)
+        cast(wq[4], W_PIECES[4][3])
+        for t in range(2):
+            for u in range(2):
+                add_up(t, u)
+        quantize_piece(wq[4])
+        main_product(3)
+
+        relu_on_scalar(0, 0)
+        relu_on_scalar(0, 1)
+        square_on_scalar(0, 0)
+        add_up(2, 0)
+        add_up(2, 1)
+        relu_on_scalar(1, 0)
+        finish_on_vector(2, 0)
+        square_on_scalar(0, 1)
+        finish_on_vector(2, 1)
+        relu_on_scalar(1, 1)
+        square_on_scalar(1, 0)
+        square_on_scalar(1, 1)
+        add_up(3, 0)
+        add_up(3, 1)
+        finish_on_vector(3, 0)
+        finish_on_vector(3, 1)

from contextlib import ExitStack

import concourse.mybir as mybir

K, R, M, N = 1024, 256, 512, 512
FLOPS = 2 * N * (K * R + K * M + R * M)

F32 = mybir.dt.float32
BF16 = mybir.dt.bfloat16
U32 = mybir.dt.uint32
U8 = mybir.dt.uint8
FP8X4 = mybir.dt.float8_e4m3fn_x4
ALU = mybir.AluOpType
ACT = mybir.ActivationFunctionType

P = 128
ROWS = 64
PACK = 4
K_PASS = P * PACK
T = 128
HALF = 256

X_PIECES = ((0, 0, HALF, 128), (1, 0, HALF, 160), (0, HALF, HALF, 160), (1, HALF, HALF, 160))
W_PIECES = ((0, 0, HALF, 192), (1, 0, HALF, HALF), (0, HALF, HALF, HALF), (1, HALF, T, T), (1, HALF + T, T, 0))
BB_ON_VECTOR = 96


def tile_rows_lora_relu2_bias_kernel(tc, x, w, a, bb, b, out):
    nc = tc.nc
    with ExitStack() as ctx:
        sb = ctx.enter_context(tc.tile_pool(name="sb", bufs=1))
        ps = ctx.enter_context(tc.psum_pool(name="ps", bufs=1))
        ctx.enter_context(tc.manual_schedule())

        def operand(name, width, code_width):
            return {
                "width": width,
                "raw": sb.tile([P, PACK, width], F32, name=name + "_raw", align_bytes=64),
                "bf16": sb.tile([P, width, PACK], BF16, name=name + "_bf16", align_bytes=64),
                "codes": sb.tile([P, code_width], U32, name=name + "_codes", align_bytes=64),
                "scales": sb.tile([P, code_width], U8, name=name + "_scales", align_bytes=64),
            }

        bbq = operand("bb", HALF, HALF)
        aq = [operand("a%d" % g, R, R + ROWS) for g in range(2)]
        xq = [operand("x%d" % i, piece[2], piece[2]) for i, piece in enumerate(X_PIECES)]
        wq = [operand("w%d" % i, piece[2], piece[2]) for i, piece in enumerate(W_PIECES)]
        bias = sb.tile([P, M // T], F32, name="bias")
        z_bf16 = [sb.tile([P, T, PACK], BF16, name="z_bf16_%d" % c, align_bytes=64) for c in range(N // T)]
        z_codes = [sb.tile([P, T], U32, name="z_codes_%d" % c, align_bytes=64) for c in range(N // T)]
        z_scales = [sb.tile([P, T], U8, name="z_scales_%d" % c, align_bytes=64) for c in range(N // T)]
        branch = [[sb.tile([P, 2, HALF], F32, name="branch%d%d" % (h, u)) for u in range(2)] for h in range(2)]
        y = [[sb.tile([P, HALF], F32, name="y%d%d" % (t, u)) for u in range(2)] for t in range(M // T)]
        relu = [[sb.tile([P, HALF], F32, name="relu%d%d" % (t, u)) for u in range(2)] for t in range(2)]
        res = [[sb.tile([P, HALF], F32, name="res%d%d" % (t, u)) for u in range(2)] for t in range(M // T)]
        whole_bank = [ps.tile([P, N], F32, name="whole%d" % c) for c in range(4)]
        half_bank = [[ps.tile([P, N], F32, name="half%d%d" % (h, u)) for u in range(2)] for h in range(2)]

        bb_rows = bb.rearrange("(p j) m -> p j m", j=PACK)
        nc.sync.dma_start(out=bbq["raw"][0:ROWS, :, :], in_=bb_rows[:, :, 0:HALF])
        nc.scalar.dma_start(out=bbq["raw"][ROWS:P, 0:3, :], in_=bb_rows[:, 1:4, HALF:M])
        nc.scalar.dma_start(out=bbq["raw"][ROWS:P, 3, :], in_=bb_rows[:, 0, HALF:M])

        def load(op, src, g, col):
            rows = src[K_PASS * g : K_PASS * (g + 1), col : col + op["width"]]
            nc.sync.dma_start(out=op["raw"][:], in_=rows.rearrange("(p j) c -> p j c", j=PACK))

        for g in range(2):
            load(aq[g], a, g, 0)
        for op, piece in zip(xq, X_PIECES):
            load(op, x, piece[0], piece[1])
        for op, piece in zip(wq, W_PIECES):
            load(op, w, piece[0], piece[1])
        with nc.allow_non_contiguous_dma(reason="one bias for each partition of an output tile"):
            nc.sync.dma_start(out=bias[:], in_=b.rearrange("(t p) o -> p (t o)", p=P))

        def scalar_copy(dst, src):
            nc.scalar.activation(out=dst, in_=src, func=ACT.Copy)

        def cast_views(op, lo, hi):
            dst = op["bf16"][:, lo:hi, :].rearrange("p (c i) j -> p c j i", i=2)
            src = op["raw"][:, :, lo:hi].rearrange("p j (c i) -> p c j i", i=2)
            return dst, src

        def cast(op, on_vector):
            if on_vector < op["width"]:
                scalar_copy(*cast_views(op, on_vector, op["width"]))
            if on_vector > 0:
                dst, src = cast_views(op, 0, on_vector)
                nc.vector.tensor_copy(out=dst, in_=src)

        def cast_a(g):
            dst = aq[g]["bf16"][:].rearrange("p (group m) j -> p m j group", group=PACK)
            src = aq[g]["raw"][:].rearrange("p j (m group) -> p m j group", group=PACK)
            scalar_copy(dst[:, :, :, 2:4], src[:, :, :, 2:4])
            nc.vector.tensor_copy(out=dst[:, :, :, 0:2], in_=src[:, :, :, 0:2])

        def quantize(codes, scales, src):
            nc.vector.quantize_mx(out=codes.bitcast(FP8X4), scales=scales, in_=src.rearrange("p c j -> p (c j)"))

        def quantize_piece(op):
            quantize(op["codes"][:], op["scales"][:], op["bf16"][:])

        def quantize_a(g):
            op = aq[g]
            quantize(op["codes"][:, 0:R], op["scales"][:, 0:R], op["bf16"][:])
            quantize(op["codes"][:, R : R + ROWS], op["scales"][:, R : R + ROWS], op["bf16"][:, 0:ROWS, :])

        def quantize_z(c):
            quantize(z_codes[c][:], z_scales[c][:], z_bf16[c][:])

        def window(ops, pieces, g, col):
            for op, piece in zip(ops, pieces):
                if piece[0] == g and piece[1] <= col < piece[1] + piece[2]:
                    cols = slice(col - piece[1], col - piece[1] + T)
                    return op["codes"][:, cols], op["scales"][:, cols]
            raise ValueError("no piece holds these columns")

        def matmul(dst, stationary, moving, start, stop):
            nc.tensor.matmul_mx(
                out=dst,
                lhsT=stationary[0].bitcast(FP8X4),
                lhsT_scale=stationary[1],
                rhs=moving[0].bitcast(FP8X4),
                rhs_scale=moving[1],
                start=start,
                stop=stop,
            )

        def z_product(c):
            for j in range(PACK):
                cols = slice(ROWS * j, ROWS * j + T)
                for g in range(2):
                    a_window = (aq[g]["codes"][:, cols], aq[g]["scales"][:, cols])
                    matmul(whole_bank[c][:, T * j : T * (j + 1)], a_window, window(xq, X_PIECES, g, T * c), g == 0, g == 1)

        def z_out(c):
            scalar_copy(z_bf16[c][:], whole_bank[c][:].rearrange("p (j n) -> p n j", j=PACK))

        def branch_product(c):
            for tile in range(2):
                cols = slice(T * tile, T * (tile + 1))
                at = HALF * tile + T * (c % 2)
                for h in range(2):
                    rows = slice(ROWS * h, ROWS * (h + 1))
                    matmul(
                        half_bank[h][c // 2][:, at : at + T],
                        (bbq["codes"][rows, cols], bbq["scales"][rows, cols]),
                        (z_codes[c][rows, :], z_scales[c][rows, :]),
                        True,
                        True,
                    )

        def branch_out(h, u):
            scalar_copy(branch[h][u][:].rearrange("p t n -> p (t n)"), half_bank[h][u][:])

        def main_product(t):
            for c in range(N // T):
                for g in range(2):
                    matmul(
                        whole_bank[t][:, T * c : T * (c + 1)],
                        window(wq, W_PIECES, g, T * t),
                        window(xq, X_PIECES, g, T * c),
                        g == 0,
                        g == 1,
                    )

        def add_up(t, u):
            nc.vector.scalar_tensor_tensor(
                out=y[t][u][:],
                in0=whole_bank[t][:, HALF * u : HALF * (u + 1)],
                scalar=bias[:, t : t + 1],
                in1=branch[t // 2][u][:, t % 2, :],
                op0=ALU.add,
                op1=ALU.add,
            )

        def store(t, u):
            nc.sync.dma_start(out=out[T * t : T * (t + 1), HALF * u : HALF * (u + 1)], in_=res[t][u][:])

        def relu_on_scalar(t, u):
            nc.scalar.activation(out=relu[t][u][:], in_=y[t][u][:], func=ACT.Relu)

        def square_on_scalar(t, u):
            nc.scalar.activation(out=res[t][u][:], in_=relu[t][u][:], func=ACT.Square)
            store(t, u)

        def finish_on_vector(t, u):
            nc.vector.scalar_tensor_tensor(
                out=res[t][u][:], in0=y[t][u][:], scalar=0.0, in1=y[t][u][:], op0=ALU.max, op1=ALU.mult
            )
            store(t, u)

        cast_a(0)
        cast(bbq, BB_ON_VECTOR)
        quantize_a(0)
        cast_a(1)
        quantize_piece(bbq)
        cast(xq[0], X_PIECES[0][3])
        quantize_a(1)
        quantize_piece(xq[0])
        cast(xq[1], X_PIECES[1][3])
        quantize_piece(xq[1])
        z_product(0)
        z_product(1)
        for i in (2, 3):
            cast(xq[i], X_PIECES[i][3])
            quantize_piece(xq[i])
        z_product(2)
        z_product(3)

        z_out(0)
        cast(wq[0], W_PIECES[0][3])
        z_out(1)
        quantize_z(0)
        quantize_piece(wq[0])
        z_out(2)
        quantize_z(1)
        cast(wq[1], W_PIECES[1][3])
        branch_product(0)
        branch_product(1)
        z_out(3)
        quantize_z(2)
        quantize_piece(wq[1])
        branch_product(2)
        quantize_z(3)
        branch_product(3)

        for u in range(2):
            for h in range(2):
                branch_out(h, u)
        cast(wq[2], W_PIECES[2][3])
        cast(wq[3], W_PIECES[3][3])
        quantize_piece(wq[2])
        quantize_piece(wq[3])
        for t in range(3):
            main_product(t)
        cast(wq[4], W_PIECES[4][3])
        for t in range(2):
            for u in range(2):
                add_up(t, u)
        quantize_piece(wq[4])
        main_product(3)

        relu_on_scalar(0, 0)
        relu_on_scalar(0, 1)
        square_on_scalar(0, 0)
        add_up(2, 0)
        add_up(2, 1)
        relu_on_scalar(1, 0)
        finish_on_vector(2, 0)
        square_on_scalar(0, 1)
        finish_on_vector(2, 1)
        relu_on_scalar(1, 1)
        square_on_scalar(1, 0)
        square_on_scalar(1, 1)
        add_up(3, 0)
        add_up(3, 1)
        finish_on_vector(3, 0)
        finish_on_vector(3, 1)
